import numpy as np
import ml_dtypes


def mxq(x, axis, fmt="e4m3"):
    dtype, down = {"e4m3": (ml_dtypes.float8_e4m3fn, 7), "e5m2": (ml_dtypes.float8_e5m2, 14)}[fmt]
    v = np.moveaxis(np.asarray(x, np.float32).astype(ml_dtypes.bfloat16).astype(np.float64), axis, -1)
    blocks = v.reshape(v.shape[:-1] + (-1, 32))
    amax = np.abs(blocks).max(-1, keepdims=True)
    byte = np.maximum(np.where(amax > 0, np.frexp(amax)[1] - 1 + 127, 0) - down, 1)
    scale = np.exp2(byte - 127.0)
    codes = (blocks / scale).astype(np.float32).astype(dtype).astype(np.float64)
    return np.moveaxis((codes * scale).reshape(v.shape), -1, axis)


WIDE = False


def mx_kscale(k):
    if not WIDE:
        return np.ones(k)
    levels = np.array([30, -30])
    if k % 512:
        return np.exp2(np.random.permutation(np.resize(levels, k // 32))).repeat(32)
    a = np.empty((k // 512, 16))
    for p in range(k // 512):
        a[p, :8] = np.random.permutation(np.resize(levels, 8))
        for g in range(8):
            far = levels[np.abs(levels - a[p, g]) >= 10]
            a[p, g + 8] = far[np.random.randint(len(far))]
    return np.exp2(a.ravel()).repeat(32)


def f64(x):
    return np.asarray(x).astype(np.float64)


def striped(idx):
    return np.tile(np.asarray(idx).reshape(-1, 16).T, (8, 1)).astype(np.uint16)


def unstriped(offs):
    return offs[:16].T.reshape(-1).astype(np.int64)


def striped8(idx):
    return np.asarray(idx).reshape(8, -1, 16).transpose(0, 2, 1).reshape(128, -1).astype(np.uint16)


def unstriped8(offs):
    return offs.reshape(8, 16, -1).transpose(0, 2, 1).reshape(8, -1).astype(np.int64)


def pick8(x, idx, run):
    r = np.arange(len(x))
    return x[r[:, None], idx[r % (8 * run) // run]]


E2M1 = np.array([0.0, 0.5, 1.0, 1.5, 2.0, 3.0, 4.0, 6.0, -0.0, -0.5, -1.0, -1.5, -2.0, -3.0, -4.0, -6.0])


def pack_weight(w, fmt):
    k, n = w.shape
    w = f64(np.asarray(w, np.float32).astype(ml_dtypes.bfloat16)).reshape(k // 32, 32, n)
    amax = np.abs(w).max(1)
    if fmt in ("e4m3", "e5m2"):
        byte = np.frexp(amax)[1] - 1 + 127 - (7 if fmt == "e4m3" else 14)
    else:
        mant, ex = np.frexp(amax / 6.0)
        byte = np.where(mant > 0.5, ex, ex - 1) + 127
    byte = np.clip(np.where(amax > 0, byte, 1), 1, 254)
    scaled = (w * np.exp2(127.0 - byte)[:, None, :]).reshape(k, n).astype(np.float32)
    by_word = np.ascontiguousarray(scaled.reshape(k // 512, 128, 4, n).transpose(0, 1, 3, 2))
    if fmt in ("e4m3", "e5m2"):
        words = by_word.astype(ml_dtypes.float8_e4m3fn if fmt == "e4m3" else ml_dtypes.float8_e5m2).view(np.uint8)
    else:
        c = by_word.astype(ml_dtypes.float4_e2m1fn).view(np.uint8) & 0xF
        words = (c[..., 0::2] | (c[..., 1::2] << 4)).reshape(k // 512, 128, 2 * n)
    return np.ascontiguousarray(words), np.ascontiguousarray(byte.astype(np.uint8).reshape(k // 512, 16, n))


def unpack_weight(words, scales, fmt):
    g, _, n = scales.shape
    words = np.ascontiguousarray(words).reshape(g, 128, n, -1)
    if fmt in ("e4m3", "e5m2"):
        vals = words.view(ml_dtypes.float8_e4m3fn if fmt == "e4m3" else ml_dtypes.float8_e5m2).astype(np.float64)
    else:
        nib = np.empty((g, 128, n, 4), np.uint8)
        nib[..., 0::2] = words & 0xF
        nib[..., 1::2] = words >> 4
        vals = E2M1[nib]
    vals = vals * np.repeat(np.exp2(scales.astype(np.float64) - 127.0), 8, axis=1)[..., None]
    return vals.transpose(0, 1, 3, 2).reshape(g * 512, n)


K, T, J, R, F, Z, C, O, N, E = 512, 1024, 256, 512, 512, 1024, 512, 128, 256, 1024


def setup_inputs():
    n = np.random.standard_normal
    idx = np.random.permutation(T)[:J]
    idx2 = np.random.permutation(Z)[:J]
    idx3 = np.stack([np.random.permutation(C)[:J] for _ in range(8)])
    idx4 = np.random.permutation(C)[:O]
    idx5 = np.random.permutation(C)[:O]
    idx6 = np.random.permutation(J)[:O]
    idx7 = np.random.permutation(E)[:O]
    fk = mx_kscale(K)
    ff = mx_kscale(F)
    fr = mx_kscale(R)
    xtp = pack_weight(n((K, T)) / fk[:, None], "e4m3")
    xop = pack_weight(n((F, Z)) / ff[:, None], "e2m1")
    wp = pack_weight(n((K, R)) * 1 / np.sqrt(K) * fk[:, None] * fr, "e2m1")
    w2p = pack_weight(n((K, R)) * 1 / np.sqrt(K) * fk[:, None] * fr, "e5m2")
    w0p = pack_weight(n((F, R)) * 1 / np.sqrt(F) * ff[:, None] * fr, "e5m2")
    wbp = pack_weight(n((R, N)) * 1 / np.sqrt(R) / fr[:, None], "e5m2")
    return {
        "xt_words": xtp[0],
        "xt_scales": xtp[1],
        "xo_words": xop[0],
        "xo_scales": xop[1],
        "w_words": wp[0],
        "w_scales": wp[1],
        "w2_words": w2p[0],
        "w2_scales": w2p[1],
        "w0_words": w0p[0],
        "w0_scales": w0p[1],
        "sa": (np.random.uniform(0.5, 1.6, (R, 1))).astype(np.float32),
        "sb": (np.random.uniform(0.5, 1.6, (R, 1))).astype(np.float32),
        "sd": (np.random.uniform(0.5, 1.6, (R, 1))).astype(np.float32),
        "wb_words": wbp[0],
        "wb_scales": wbp[1],
        "offs": striped(idx),
        "offs2": striped(idx2),
        "offs3": striped8(idx3),
        "offs4": striped(idx4),
        "offs5": striped(idx5),
        "offs6": striped(idx6),
        "offs7": striped(idx7),
    }


def reference(xt_words, xt_scales, xo_words, xo_scales, w_words, w_scales, w2_words, w2_scales, w0_words, w0_scales, sa, sb, sd, wb_words, wb_scales, offs, offs2, offs3, offs4, offs5, offs6, offs7):
    idx = unstriped(offs)
    idx2 = unstriped(offs2)
    idx3 = unstriped8(offs3)
    idx4 = unstriped(offs4)
    idx5 = unstriped(offs5)
    idx6 = unstriped(offs6)
    idx7 = unstriped(offs7)
    xtu = unpack_weight(xt_words, xt_scales, "e4m3")
    xou = unpack_weight(xo_words, xo_scales, "e2m1")
    wu = unpack_weight(w_words, w_scales, "e2m1")
    w2u = unpack_weight(w2_words, w2_scales, "e5m2")
    w0u = unpack_weight(w0_words, w0_scales, "e5m2")
    wbu = unpack_weight(wb_words, wb_scales, "e5m2")
    xtidxg = xtu[:, idx]
    a = wu.T @ xtidxg
    xoidx2g = xou[:, idx2]
    b = w2u.T @ xtidxg + w0u.T @ xoidx2g
    pw = np.zeros((R, C))
    pw[np.arange(R)[:, None], idx3[np.arange(R) % 512 // 64]] = a
    hid = np.maximum(pw[:, idx4] * f64(sa), pw[:, idx5] * f64(sb)) - b[:, idx6] * f64(sd)
    hidq = mxq(hid, 0, "e4m3")
    p = wbu.T @ hidq
    y = np.zeros((N, E))
    y[:, idx7] = p
    return y

@@ -1,0 +1,185 @@
+from contextlib import ExitStack
+
+import concourse.mybir as mybir
+
+K, T, J, R, F, Z, C, O, N, E = 512, 1024, 256, 512, 512, 1024, 512, 128, 256, 1024
+FLOPS = 2 * (3 * K * R * J + R * N * O)
+
+F32 = mybir.dt.float32
+BF16 = mybir.dt.bfloat16
+I32 = mybir.dt.int32
+U32 = mybir.dt.uint32
+U16 = mybir.dt.uint16
+U8 = mybir.dt.uint8
+E4M3 = mybir.dt.float8_e4m3fn_x4
+E5M2 = mybir.dt.float8_e5m2_x4
+E2M1 = mybir.dt.float4_e2m1fn_x4
+COPY = mybir.ActivationFunctionType.Copy
+MAX = mybir.AluOpType.max
+SUB = mybir.AluOpType.subtract
+
+P = 128
+PACK = 4
+QUADS = 4
+LINE = 16
+
+
+def tile_list_ownthree_leaned_one_scattered_kernel(
+    tc, xt_words, xt_scales, xo_words, xo_scales, w_words, w_scales, w2_words, w2_scales, w0_words, w0_scales,
+    sa, sb, sd, wb_words, wb_scales, offs, offs2, offs3, offs4, offs5, offs6, offs7, out,
+):
+    nc = tc.nc
+    with ExitStack() as ctx:
+        keep = ctx.enter_context(tc.tile_pool(name="keep", bufs=1))
+        psum = ctx.enter_context(tc.psum_pool(name="psum", bufs=1))
+
+        def sbuf(name, shape, dtype, tag=None):
+            return keep.tile(shape, dtype, name=name, tag=tag or name, align_bytes=64)
+
+        def load_list(name, src):
+            lst = keep.tile(list(src.shape), U16, name=name)
+            nc.sync.dma_start(lst[:], src)
+            return lst
+
+        def load_words(name, src, cols, dtype):
+            words = sbuf(name, [P, cols], dtype)
+            rows = src[0] if src.ndim == 3 else src[0].rearrange("p n t -> p (n t)")
+            nc.sync.dma_start(words[:].bitcast(I32), rows.bitcast(I32))
+            return words
+
+        def load_plane(name, src, cols):
+            plane = sbuf(name, [P, cols], U8)
+            rows = src[0].bitcast(I32)
+            for q in range(QUADS):
+                nc.sync.dma_start(
+                    plane[32 * q : 32 * q + 32, :].bitcast(I32),
+                    rows[4 * q : 4 * q + 4, :].partition_broadcast(8),
+                )
+            return plane
+
+        def load_factor(name, src):
+            factor = keep.tile([P, PACK], F32, name=name)
+            nc.sync.dma_start(factor[:], src.rearrange("(p t) one -> p (t one)", t=PACK))
+            return factor
+
+        def deal(copy, name, raw, dtype, run):
+            dealt = sbuf(name, [P, PACK, P], dtype)
+            copy(dealt[:].rearrange("p t (c i) -> p c t i", i=run), raw[:].rearrange("p (c i t) -> p c t i", i=run, t=PACK))
+            return dealt
+
+        def pick(name, table, lst, dtype):
+            picked = sbuf(name, [P, J], dtype)
+            nc.vector.tensor_copy(picked[:], table[:].indirect(lst[:]))
+            return picked
+
+        l_tok = load_list("l_tok", offs)
+        xt_s = load_plane("xt_s", xt_scales, T)
+        xt_w = load_words("xt_w", xt_words, T, U32)
+        w_w = load_words("w_w", w_words, R, U16)
+        w_s = load_plane("w_s", w_scales, R)
+        l_board = load_list("l_board", offs3)
+        l_first = load_list("l_first", offs4)
+        l_second = load_list("l_second", offs5)
+        sa_t = load_factor("sa_t", sa)
+        sb_t = load_factor("sb_t", sb)
+        l_note = load_list("l_note", offs2)
+        xo_s = load_plane("xo_s", xo_scales, Z)
+        xo_w = load_words("xo_w", xo_words, Z, U16)
+        w2_w = load_words("w2_w", w2_words, R, U32)
+        w2_s = load_plane("w2_s", w2_scales, R)
+        w0_w = load_words("w0_w", w0_words, R, U32)
+        w0_s = load_plane("w0_s", w0_scales, R)
+        l_slot = load_list("l_slot", offs6)
+        sd_t = load_factor("sd_t", sd)
+        wb_w = load_words("wb_w", wb_words, N, U32)
+        wb_s = load_plane("wb_s", wb_scales, N)
+        l_page = load_list("l_page", offs7)
+
+        boards = [sbuf("board%d" % t, [P, C], F32) for t in range(PACK)]
+        pages = [sbuf("page%d" % h, [P, E], F32) for h in range(N // P)]
+        for zeroed in boards + pages:
+            nc.vector.memset(zeroed[:], 0.0)
+
+        xg_s = pick("xg_s", xt_s, l_tok, U8)
+        xg_w = pick("xg_w", xt_w, l_tok, U32)
+        wd_w = deal(nc.scalar.copy, "wd_w", w_w, U16, LINE // 2)
+        wd_s = deal(nc.vector.tensor_copy, "wd_s", w_s, U8, LINE)
+
+        a_banks = [psum.tile([P, J], F32, name="a_bank0"), psum.tile([P, J], F32, name="a_bank1")]
+        a_pair = psum.tile([P, 2, J], F32, name="a_pair")
+        a_ps = [a_banks[0][:], a_banks[1][:], a_pair[:, 0, :], a_pair[:, 1, :]]
+        for t in range(PACK):
+            nc.tensor.matmul_mx(
+                out=a_ps[t], lhsT=wd_w[:, t, :].bitcast(E2M1), lhsT_scale=wd_s[:, t, :],
+                rhs=xg_w[:].bitcast(E4M3), rhs_scale=xg_s[:], start=True, stop=True,
+            )
+        a_sb = [sbuf("a_sb0", [P, J], F32), sbuf("a_sb1", [P, J], F32)]
+        a_sb_pair = sbuf("a_sb_pair", [P, 2, J], F32)
+        nc.vector.tensor_copy(a_sb[0][:], a_ps[0])
+        nc.vector.tensor_copy(a_sb[1][:], a_ps[1])
+        nc.vector.tensor_copy(a_sb_pair[:], a_pair[:])
+        a_rows = [a_sb[0][:], a_sb[1][:], a_sb_pair[:, 0, :], a_sb_pair[:, 1, :]]
+        for t in range(PACK):
+            nc.scalar.activation(boards[t][:].indirect(l_board[:]), a_rows[t], COPY)
+
+        first = sbuf("first", [P, PACK, O], F32)
+        second = sbuf("second", [P, PACK, O], F32)
+        for t in range(PACK):
+            nc.scalar.activation(first[:, t, :], boards[t][:].indirect(l_first[:]), COPY, scale=sa_t[:, t : t + 1])
+            nc.scalar.activation(second[:, t, :], boards[t][:].indirect(l_second[:]), COPY, scale=sb_t[:, t : t + 1])
+
+        og_s = pick("og_s", xo_s, l_note, U8)
+        og_w = pick("og_w", xo_w, l_note, U16)
+        w2d_w = deal(nc.vector.tensor_copy, "w2d_w", w2_w, U32, LINE // 4)
+        w2d_s = deal(nc.vector.tensor_copy, "w2d_s", w2_s, U8, LINE)
+        w0d_w = deal(nc.vector.tensor_copy, "w0d_w", w0_w, U32, LINE // 4)
+        w0d_s = deal(nc.vector.tensor_copy, "w0d_s", w0_s, U8, LINE)
+
+        b_banks = [psum.tile([P, 2, J], F32, name="b_bank%d" % u) for u in range(2)]
+        for t in range(PACK):
+            b_ps = b_banks[t // 2][:, t % 2, :]
+            nc.tensor.matmul_mx(
+                out=b_ps, lhsT=w2d_w[:, t, :].bitcast(E5M2), lhsT_scale=w2d_s[:, t, :],
+                rhs=xg_w[:].bitcast(E4M3), rhs_scale=xg_s[:], start=True, stop=False,
+            )
+            nc.tensor.matmul_mx(
+                out=b_ps, lhsT=w0d_w[:, t, :].bitcast(E5M2), lhsT_scale=w0d_s[:, t, :],
+                rhs=og_w[:].bitcast(E2M1), rhs_scale=og_s[:], start=False, stop=True,
+            )
+        b_rows = [sbuf("b_rows%d" % t, [P, J], F32) for t in range(PACK)]
+        for t in range(PACK):
+            nc.vector.tensor_copy(b_rows[t][:], b_banks[t // 2][:, t % 2, :])
+
+        larger = sbuf("larger", [P, PACK, O], F32, tag="w0d_w")
+        for u in range(2):
+            ts = slice(2 * u, 2 * u + 2)
+            nc.vector.tensor_tensor(larger[:, ts, :], first[:, ts, :], second[:, ts, :], MAX)
+
+        third = sbuf("third", [P, PACK, O], F32)
+        for t in range(PACK):
+            nc.scalar.activation(third[:, t, :], b_rows[t][:].indirect(l_slot[:]), COPY, scale=sd_t[:, t : t + 1])
+
+        hid = sbuf("hid", [P, O, PACK], BF16)
+        for u in range(2):
+            ts = slice(2 * u, 2 * u + 2)
+            nc.vector.tensor_tensor(
+                hid[:, :, ts], larger[:, ts, :].rearrange("p t o -> p o t"), third[:, ts, :].rearrange("p t o -> p o t"), SUB
+            )
+        hid_w = sbuf("hid_w", [P, O], U32)
+        hid_s = sbuf("hid_s", [P, O], U8)
+        nc.vector.quantize_mx(out=hid_w[:].bitcast(E4M3), scales=hid_s[:], in_=hid[:].rearrange("p o t -> p (o t)"))
+
+        p_banks = [psum.tile([P, O], F32, name="p_bank%d" % h) for h in range(N // P)]
+        p_rows = [sbuf("p_rows%d" % h, [P, O], F32) for h in range(N // P)]
+        for h in range(N // P):
+            cols = slice(h * P, (h + 1) * P)
+            nc.tensor.matmul_mx(
+                out=p_banks[h][:], lhsT=wb_w[:, cols].bitcast(E5M2), lhsT_scale=wb_s[:, cols],
+                rhs=hid_w[:].bitcast(E4M3), rhs_scale=hid_s[:], start=True, stop=True,
+            )
+        nc.scalar.copy(p_rows[0][:], p_banks[0][:])
+        nc.scalar.activation(pages[0][:].indirect(l_page[:]), p_rows[0][:], COPY)
+        nc.vector.tensor_copy(p_rows[1][:], p_banks[1][:])
+        nc.vector.tensor_copy(pages[1][:].indirect(l_page[:]), p_rows[1][:])
+        for h in range(N // P):
+            nc.sync.dma_start(out[h * P : (h + 1) * P, :], pages[h][:])

@@ -72,11 +72,12 @@ def tile_list_ownthree_leaned_one_scattered_kernel(
             nc.vector.tensor_copy(picked[:], table[:].indirect(lst[:]))
             return picked
 
-        l_tok = load_list("l_tok", offs)
-        xt_s = load_plane("xt_s", xt_scales, T)
+        w_stage = sbuf("w_stage", [4, QUADS, R // 4], I32)
+        nc.sync.dma_start(w_stage[:], w_scales[0].bitcast(I32).rearrange("(q r) c -> r q c", q=QUADS))
         xt_w = load_words("xt_w", xt_words, T, U32)
+        l_tok = load_list("l_tok", offs)
         w_w = load_words("w_w", w_words, R, U16)
-        w_s = load_plane("w_s", w_scales, R)
+        xt_s = load_plane("xt_s", xt_scales, T)
         l_board = load_list("l_board", offs3)
         l_first = load_list("l_first", offs4)
         l_second = load_list("l_second", offs5)
@@ -96,31 +97,68 @@ def tile_list_ownthree_leaned_one_scattered_kernel(
         l_page = load_list("l_page", offs7)
 
         boards = [sbuf("board%d" % t, [P, C], F32) for t in range(PACK)]
-        pages = [sbuf("page%d" % h, [P, E], F32) for h in range(N // P)]
+        w_s = sbuf("w_s", [P, R], U8)
+        nc.vector.memset(w_s[:].bitcast(I32), 0)
+        pages = [sbuf("page0", [P, E], F32)]
         for zeroed in boards + pages:
-            nc.vector.memset(zeroed[:], 0.0)
+            nc.vector.memset(zeroed[:].bitcast(I32), 0)
+        for q in range(QUADS):
+            nc.vector.tensor_copy(w_s[32 * q : 32 * q + 4, :].bitcast(I32), w_stage[:, q, :])
 
-        xg_s = pick("xg_s", xt_s, l_tok, U8)
-        xg_w = pick("xg_w", xt_w, l_tok, U32)
-        wd_w = deal(nc.scalar.copy, "wd_w", w_w, U16, LINE // 2)
-        wd_s = deal(nc.vector.tensor_copy, "wd_s", w_s, U8, LINE)
+        wd_w = sbuf("wd_w", [P, PACK, P], U16)
+        wd_s = sbuf("wd_s", [P, PACK, P], U8)
+        xg_w = sbuf("xg_w", [P, J], U32)
+        xg_s = sbuf("xg_s", [P, J], U8)
+        half = J // 2
+        halves = [slice(0, half), slice(half, J)]
+        half_lists = [slice(0, half // 16), slice(half // 16, J // 16)]
 
-        a_banks = [psum.tile([P, J], F32, name="a_bank0"), psum.tile([P, J], F32, name="a_bank1")]
-        a_pair = psum.tile([P, 2, J], F32, name="a_pair")
-        a_ps = [a_banks[0][:], a_banks[1][:], a_pair[:, 0, :], a_pair[:, 1, :]]
-        for t in range(PACK):
-            nc.tensor.matmul_mx(
-                out=a_ps[t], lhsT=wd_w[:, t, :].bitcast(E2M1), lhsT_scale=wd_s[:, t, :],
-                rhs=xg_w[:].bitcast(E4M3), rhs_scale=xg_s[:], start=True, stop=True,
+        def deal_part(copy, dealt, raw, run, ts):
+            copy(
+                dealt[:, ts, :].rearrange("p t (c i) -> p c t i", i=run),
+                raw[:].rearrange("p (c i t) -> p c t i", i=run, t=PACK)[:, :, ts, :],
             )
-        a_sb = [sbuf("a_sb0", [P, J], F32), sbuf("a_sb1", [P, J], F32)]
-        a_sb_pair = sbuf("a_sb_pair", [P, 2, J], F32)
-        nc.vector.tensor_copy(a_sb[0][:], a_ps[0])
-        nc.vector.tensor_copy(a_sb[1][:], a_ps[1])
-        nc.vector.tensor_copy(a_sb_pair[:], a_pair[:])
-        a_rows = [a_sb[0][:], a_sb[1][:], a_sb_pair[:, 0, :], a_sb_pair[:, 1, :]]
-        for t in range(PACK):
-            nc.scalar.activation(boards[t][:].indirect(l_board[:]), a_rows[t], COPY)
+
+        def pick_half(picked, table, u):
+            nc.vector.tensor_copy(picked[:, halves[u]], table[:].indirect(l_tok[:, half_lists[u]]))
+
+        def first_product(dst, t, cols):
+            nc.tensor.matmul_mx(
+                out=dst, lhsT=wd_w[:, t, :].bitcast(E2M1), lhsT_scale=wd_s[:, t, :],
+                rhs=xg_w[:, cols].bitcast(E4M3), rhs_scale=xg_s[:, cols], start=True, stop=True,
+            )
+
+        deal_part(nc.vector.tensor_copy, wd_s, w_s, LINE, slice(0, 2))
+        pick_half(xg_w, xt_w, 0)
+        pick_half(xg_s, xt_s, 0)
+        deal_part(nc.scalar.copy, wd_w, w_w, LINE // 2, slice(0, 1))
+        deal_part(nc.scalar.copy, wd_w, w_w, LINE // 2, slice(1, PACK))
+
+        a_early = [psum.tile([P, half], F32, name="a_early%d" % t) for t in range(2)]
+        a_next = psum.tile([P, 2, half], F32, name="a_next")
+        a_late = psum.tile([P, 2, J], F32, name="a_late")
+        r_early = [sbuf("r_early%d" % t, [P, half], F32) for t in range(2)]
+        r_next = sbuf("r_next", [P, 2, half], F32)
+        r_late = sbuf("r_late", [P, 2, J], F32)
+        for t in range(2):
+            first_product(a_early[t][:], t, halves[0])
+        nc.scalar.copy(r_early[0][:], a_early[0][:])
+        nc.scalar.activation(boards[0][:].indirect(l_board[:, half_lists[0]]), r_early[0][:], COPY)
+        pick_half(xg_s, xt_s, 1)
+        nc.vector.tensor_copy(r_early[1][:], a_early[1][:])
+        nc.scalar.activation(boards[1][:].indirect(l_board[:, half_lists[0]]), r_early[1][:], COPY)
+        pick_half(xg_w, xt_w, 1)
+        for t in range(2):
+            first_product(a_next[:, t, :], t, halves[1])
+        deal_part(nc.vector.tensor_copy, wd_s, w_s, LINE, slice(2, PACK))
+        nc.vector.tensor_copy(r_next[:], a_next[:])
+        for t in range(2):
+            nc.scalar.activation(boards[t][:].indirect(l_board[:, half_lists[1]]), r_next[:, t, :], COPY)
+        for t in range(2, PACK):
+            first_product(a_late[:, t - 2, :], t, slice(0, J))
+        nc.vector.tensor_copy(r_late[:], a_late[:])
+        for t in range(2, PACK):
+            nc.scalar.activation(boards[t][:].indirect(l_board[:]), r_late[:, t - 2, :], COPY)
 
         first = sbuf("first", [P, PACK, O], F32)
         second = sbuf("second", [P, PACK, O], F32)
@@ -137,18 +175,21 @@ def tile_list_ownthree_leaned_one_scattered_kernel(
 
         b_banks = [psum.tile([P, 2, J], F32, name="b_bank%d" % u) for u in range(2)]
         for t in range(PACK):
-            b_ps = b_banks[t // 2][:, t % 2, :]
             nc.tensor.matmul_mx(
-                out=b_ps, lhsT=w2d_w[:, t, :].bitcast(E5M2), lhsT_scale=w2d_s[:, t, :],
-                rhs=xg_w[:].bitcast(E4M3), rhs_scale=xg_s[:], start=True, stop=False,
+                out=b_banks[t // 2][:, t % 2, :], lhsT=w2d_w[:, t, :].bitcast(E5M2), lhsT_scale=w2d_s[:, t, :],
+                rhs=xg_w[:].bitcast(E4M3), rhs_scale=xg_s[:], start=(t % 2 == 0), stop=False,
             )
+        for t in range(PACK):
             nc.tensor.matmul_mx(
-                out=b_ps, lhsT=w0d_w[:, t, :].bitcast(E5M2), lhsT_scale=w0d_s[:, t, :],
-                rhs=og_w[:].bitcast(E2M1), rhs_scale=og_s[:], start=False, stop=True,
+                out=b_banks[t // 2][:, t % 2, :], lhsT=w0d_w[:, t, :].bitcast(E5M2), lhsT_scale=w0d_s[:, t, :],
+                rhs=og_w[:].bitcast(E2M1), rhs_scale=og_s[:], start=False, stop=(t % 2 == 1),
             )
         b_rows = [sbuf("b_rows%d" % t, [P, J], F32) for t in range(PACK)]
         for t in range(PACK):
             nc.vector.tensor_copy(b_rows[t][:], b_banks[t // 2][:, t % 2, :])
+
+        pages.append(sbuf("page1", [P, E], F32, tag="w0d_s"))
+        nc.vector.memset(pages[1][:].bitcast(I32), 0)
 
         larger = sbuf("larger", [P, PACK, O], F32, tag="w0d_w")
         for u in range(2):

@@ -97,13 +97,14 @@ def tile_list_ownthree_leaned_one_scattered_kernel(
         l_page = load_list("l_page", offs7)
 
         boards = [sbuf("board%d" % t, [P, C], F32) for t in range(PACK)]
-        w_s = sbuf("w_s", [P, R], U8)
-        nc.vector.memset(w_s[:].bitcast(I32), 0)
-        pages = [sbuf("page0", [P, E], F32)]
-        for zeroed in boards + pages:
+        w_two = sbuf("w_two", [P, 2, R // 4], I32)
+        nc.vector.memset(w_two[:], 0)
+        for zeroed in boards:
             nc.vector.memset(zeroed[:].bitcast(I32), 0)
-        for q in range(QUADS):
-            nc.vector.tensor_copy(w_s[32 * q : 32 * q + 4, :].bitcast(I32), w_stage[:, q, :])
+        for q in range(2):
+            nc.vector.tensor_copy(w_two[32 * q : 32 * q + 4, :, :], w_stage[:, q:QUADS:2, :])
+        nc.vector.tensor_copy(w_two[64:P, 0, :], w_two[0:64, 1, :])
+        w_s = w_two[:, 0, :].bitcast(U8)
 
         wd_w = sbuf("wd_w", [P, PACK, P], U16)
         wd_s = sbuf("wd_s", [P, PACK, P], U8)
@@ -116,7 +117,7 @@ def tile_list_ownthree_leaned_one_scattered_kernel(
         def deal_part(copy, dealt, raw, run, ts):
             copy(
                 dealt[:, ts, :].rearrange("p t (c i) -> p c t i", i=run),
-                raw[:].rearrange("p (c i t) -> p c t i", i=run, t=PACK)[:, :, ts, :],
+                raw.rearrange("p (c i t) -> p c t i", i=run, t=PACK)[:, :, ts, :],
             )
 
         def pick_half(picked, table, u):
@@ -131,8 +132,8 @@ def tile_list_ownthree_leaned_one_scattered_kernel(
         deal_part(nc.vector.tensor_copy, wd_s, w_s, LINE, slice(0, 2))
         pick_half(xg_w, xt_w, 0)
         pick_half(xg_s, xt_s, 0)
-        deal_part(nc.scalar.copy, wd_w, w_w, LINE // 2, slice(0, 1))
-        deal_part(nc.scalar.copy, wd_w, w_w, LINE // 2, slice(1, PACK))
+        deal_part(nc.scalar.copy, wd_w, w_w[:], LINE // 2, slice(0, 1))
+        deal_part(nc.scalar.copy, wd_w, w_w[:], LINE // 2, slice(1, PACK))
 
         a_early = [psum.tile([P, half], F32, name="a_early%d" % t) for t in range(2)]
         a_next = psum.tile([P, 2, half], F32, name="a_next")
@@ -188,8 +189,9 @@ def tile_list_ownthree_leaned_one_scattered_kernel(
         for t in range(PACK):
             nc.vector.tensor_copy(b_rows[t][:], b_banks[t // 2][:, t % 2, :])
 
-        pages.append(sbuf("page1", [P, E], F32, tag="w0d_s"))
-        nc.vector.memset(pages[1][:].bitcast(I32), 0)
+        pages = [sbuf("page%d" % h, [P, E], F32, tag=tag) for h, tag in enumerate(("w2_w", "w0d_s"))]
+        for zeroed in pages:
+            nc.vector.memset(zeroed[:].bitcast(I32), 0)
 
         larger = sbuf("larger", [P, PACK, O], F32, tag="w0d_w")
         for u in range(2):
@@ -197,15 +199,26 @@ def tile_list_ownthree_leaned_one_scattered_kernel(
             nc.vector.tensor_tensor(larger[:, ts, :], first[:, ts, :], second[:, ts, :], MAX)
 
         third = sbuf("third", [P, PACK, O], F32)
-        for t in range(PACK):
-            nc.scalar.activation(third[:, t, :], b_rows[t][:].indirect(l_slot[:]), COPY, scale=sd_t[:, t : t + 1])
-
         hid = sbuf("hid", [P, O, PACK], BF16)
-        for u in range(2):
-            ts = slice(2 * u, 2 * u + 2)
+
+        def look_up_b(t, places):
+            entries = l_slot[:, places.start // 16 : places.stop // 16]
+            nc.scalar.activation(third[:, t, places], b_rows[t][:].indirect(entries), COPY, scale=sd_t[:, t : t + 1])
+
+        def take_off(ts, places):
             nc.vector.tensor_tensor(
-                hid[:, :, ts], larger[:, ts, :].rearrange("p t o -> p o t"), third[:, ts, :].rearrange("p t o -> p o t"), SUB
+                hid[:, places, ts],
+                larger[:, ts, places].rearrange("p t o -> p o t"),
+                third[:, ts, places].rearrange("p t o -> p o t"),
+                SUB,
             )
+
+        for t in range(PACK - 1):
+            look_up_b(t, slice(0, O))
+        take_off(slice(0, 2), slice(0, O))
+        for places in (slice(0, O // 2), slice(O // 2, O)):
+            look_up_b(PACK - 1, places)
+            take_off(slice(2, PACK), places)
         hid_w = sbuf("hid_w", [P, O], U32)
         hid_s = sbuf("hid_s", [P, O], U8)
         nc.vector.quantize_mx(out=hid_w[:].bitcast(E4M3), scales=hid_s[:], in_=hid[:].rearrange("p o t -> p (o t)"))
@@ -222,5 +235,5 @@ def tile_list_ownthree_leaned_one_scattered_kernel(
         nc.scalar.activation(pages[0][:].indirect(l_page[:]), p_rows[0][:], COPY)
         nc.vector.tensor_copy(p_rows[1][:], p_banks[1][:])
         nc.vector.tensor_copy(pages[1][:].indirect(l_page[:]), p_rows[1][:])
-        for h in range(N // P):
-            nc.sync.dma_start(out[h * P : (h + 1) * P, :], pages[h][:])
+        for h, queue in enumerate((nc.scalar, nc.sync)):
+            queue.dma_start(out[h * P : (h + 1) * P, :], pages[h][:])

from contextlib import ExitStack

import concourse.mybir as mybir

K, T, J, R, F, Z, C, O, N, E = 512, 1024, 256, 512, 512, 1024, 512, 128, 256, 1024
FLOPS = 2 * (3 * K * R * J + R * N * O)

F32 = mybir.dt.float32
BF16 = mybir.dt.bfloat16
I32 = mybir.dt.int32
U32 = mybir.dt.uint32
U16 = mybir.dt.uint16
U8 = mybir.dt.uint8
E4M3 = mybir.dt.float8_e4m3fn_x4
E5M2 = mybir.dt.float8_e5m2_x4
E2M1 = mybir.dt.float4_e2m1fn_x4
COPY = mybir.ActivationFunctionType.Copy
MAX = mybir.AluOpType.max
SUB = mybir.AluOpType.subtract

P = 128
PACK = 4
QUADS = 4
LINE = 16


def tile_list_ownthree_leaned_one_scattered_kernel(
    tc, xt_words, xt_scales, xo_words, xo_scales, w_words, w_scales, w2_words, w2_scales, w0_words, w0_scales,
    sa, sb, sd, wb_words, wb_scales, offs, offs2, offs3, offs4, offs5, offs6, offs7, out,
):
    nc = tc.nc
    with ExitStack() as ctx:
        keep = ctx.enter_context(tc.tile_pool(name="keep", bufs=1))
        psum = ctx.enter_context(tc.psum_pool(name="psum", bufs=1))

        def sbuf(name, shape, dtype, tag=None):
            return keep.tile(shape, dtype, name=name, tag=tag or name, align_bytes=64)

        def load_list(name, src):
            lst = keep.tile(list(src.shape), U16, name=name)
            nc.sync.dma_start(lst[:], src)
            return lst

        def load_words(name, src, cols, dtype):
            words = sbuf(name, [P, cols], dtype)
            rows = src[0] if src.ndim == 3 else src[0].rearrange("p n t -> p (n t)")
            nc.sync.dma_start(words[:].bitcast(I32), rows.bitcast(I32))
            return words

        def load_plane(name, src, cols):
            plane = sbuf(name, [P, cols], U8)
            rows = src[0].bitcast(I32)
            for q in range(QUADS):
                nc.sync.dma_start(
                    plane[32 * q : 32 * q + 32, :].bitcast(I32),
                    rows[4 * q : 4 * q + 4, :].partition_broadcast(8),
                )
            return plane

        def load_factor(name, src):
            factor = keep.tile([P, PACK], F32, name=name)
            nc.sync.dma_start(factor[:], src.rearrange("(p t) one -> p (t one)", t=PACK))
            return factor

        def deal(copy, name, raw, dtype, run):
            dealt = sbuf(name, [P, PACK, P], dtype)
            copy(dealt[:].rearrange("p t (c i) -> p c t i", i=run), raw[:].rearrange("p (c i t) -> p c t i", i=run, t=PACK))
            return dealt

        def pick(name, table, lst, dtype):
            picked = sbuf(name, [P, J], dtype)
            nc.vector.tensor_copy(picked[:], table[:].indirect(lst[:]))
            return picked

        w_stage = sbuf("w_stage", [4, QUADS, R // 4], I32)
        nc.sync.dma_start(w_stage[:], w_scales[0].bitcast(I32).rearrange("(q r) c -> r q c", q=QUADS))
        xt_w = load_words("xt_w", xt_words, T, U32)
        l_tok = load_list("l_tok", offs)
        w_w = load_words("w_w", w_words, R, U16)
        xt_s = load_plane("xt_s", xt_scales, T)
        l_board = load_list("l_board", offs3)
        l_first = load_list("l_first", offs4)
        l_second = load_list("l_second", offs5)
        sa_t = load_factor("sa_t", sa)
        sb_t = load_factor("sb_t", sb)
        l_note = load_list("l_note", offs2)
        xo_s = load_plane("xo_s", xo_scales, Z)
        xo_w = load_words("xo_w", xo_words, Z, U16)
        w2_w = load_words("w2_w", w2_words, R, U32)
        w2_s = load_plane("w2_s", w2_scales, R)
        w0_w = load_words("w0_w", w0_words, R, U32)
        w0_s = load_plane("w0_s", w0_scales, R)
        l_slot = load_list("l_slot", offs6)
        sd_t = load_factor("sd_t", sd)
        wb_w = load_words("wb_w", wb_words, N, U32)
        wb_s = load_plane("wb_s", wb_scales, N)
        l_page = load_list("l_page", offs7)

        boards = [sbuf("board%d" % t, [P, C], F32) for t in range(PACK)]
        w_two = sbuf("w_two", [P, 2, R // 4], I32)
        nc.vector.memset(w_two[:], 0)
        for zeroed in boards:
            nc.vector.memset(zeroed[:].bitcast(I32), 0)
        for q in range(2):
            nc.vector.tensor_copy(w_two[32 * q : 32 * q + 4, :, :], w_stage[:, q:QUADS:2, :])
        nc.vector.tensor_copy(w_two[64:P, 0, :], w_two[0:64, 1, :])
        w_s = w_two[:, 0, :].bitcast(U8)

        wd_w = sbuf("wd_w", [P, PACK, P], U16)
        wd_s = sbuf("wd_s", [P, PACK, P], U8)
        xg_w = sbuf("xg_w", [P, J], U32)
        xg_s = sbuf("xg_s", [P, J], U8)
        half = J // 2
        halves = [slice(0, half), slice(half, J)]
        half_lists = [slice(0, half // 16), slice(half // 16, J // 16)]

        def deal_part(copy, dealt, raw, run, ts):
            copy(
                dealt[:, ts, :].rearrange("p t (c i) -> p c t i", i=run),
                raw.rearrange("p (c i t) -> p c t i", i=run, t=PACK)[:, :, ts, :],
            )

        def pick_half(picked, table, u):
            nc.vector.tensor_copy(picked[:, halves[u]], table[:].indirect(l_tok[:, half_lists[u]]))

        def first_product(dst, t, cols):
            nc.tensor.matmul_mx(
                out=dst, lhsT=wd_w[:, t, :].bitcast(E2M1), lhsT_scale=wd_s[:, t, :],
                rhs=xg_w[:, cols].bitcast(E4M3), rhs_scale=xg_s[:, cols], start=True, stop=True,
            )

        deal_part(nc.vector.tensor_copy, wd_s, w_s, LINE, slice(0, 2))
        pick_half(xg_w, xt_w, 0)
        pick_half(xg_s, xt_s, 0)
        deal_part(nc.scalar.copy, wd_w, w_w[:], LINE // 2, slice(0, 1))
        deal_part(nc.scalar.copy, wd_w, w_w[:], LINE // 2, slice(1, PACK))

        a_early = [psum.tile([P, half], F32, name="a_early%d" % t) for t in range(2)]
        a_next = psum.tile([P, 2, half], F32, name="a_next")
        a_late = psum.tile([P, 2, J], F32, name="a_late")
        r_early = [sbuf("r_early%d" % t, [P, half], F32) for t in range(2)]
        r_next = sbuf("r_next", [P, 2, half], F32)
        r_late = sbuf("r_late", [P, 2, J], F32)
        for t in range(2):
            first_product(a_early[t][:], t, halves[0])
        nc.scalar.copy(r_early[0][:], a_early[0][:])
        nc.scalar.activation(boards[0][:].indirect(l_board[:, half_lists[0]]), r_early[0][:], COPY)
        pick_half(xg_s, xt_s, 1)
        nc.vector.tensor_copy(r_early[1][:], a_early[1][:])
        nc.scalar.activation(boards[1][:].indirect(l_board[:, half_lists[0]]), r_early[1][:], COPY)
        pick_half(xg_w, xt_w, 1)
        for t in range(2):
            first_product(a_next[:, t, :], t, halves[1])
        deal_part(nc.vector.tensor_copy, wd_s, w_s, LINE, slice(2, PACK))
        nc.vector.tensor_copy(r_next[:], a_next[:])
        for t in range(2):
            nc.scalar.activation(boards[t][:].indirect(l_board[:, half_lists[1]]), r_next[:, t, :], COPY)
        for t in range(2, PACK):
            first_product(a_late[:, t - 2, :], t, slice(0, J))
        nc.vector.tensor_copy(r_late[:], a_late[:])
        for t in range(2, PACK):
            nc.scalar.activation(boards[t][:].indirect(l_board[:]), r_late[:, t - 2, :], COPY)

        first = sbuf("first", [P, PACK, O], F32)
        second = sbuf("second", [P, PACK, O], F32)
        for t in range(PACK):
            nc.scalar.activation(first[:, t, :], boards[t][:].indirect(l_first[:]), COPY, scale=sa_t[:, t : t + 1])
            nc.scalar.activation(second[:, t, :], boards[t][:].indirect(l_second[:]), COPY, scale=sb_t[:, t : t + 1])

        og_s = pick("og_s", xo_s, l_note, U8)
        og_w = pick("og_w", xo_w, l_note, U16)
        w2d_w = deal(nc.vector.tensor_copy, "w2d_w", w2_w, U32, LINE // 4)
        w2d_s = deal(nc.vector.tensor_copy, "w2d_s", w2_s, U8, LINE)
        w0d_w = deal(nc.vector.tensor_copy, "w0d_w", w0_w, U32, LINE // 4)
        w0d_s = deal(nc.vector.tensor_copy, "w0d_s", w0_s, U8, LINE)

        b_banks = [psum.tile([P, 2, J], F32, name="b_bank%d" % u) for u in range(2)]
        for t in range(PACK):
            nc.tensor.matmul_mx(
                out=b_banks[t // 2][:, t % 2, :], lhsT=w2d_w[:, t, :].bitcast(E5M2), lhsT_scale=w2d_s[:, t, :],
                rhs=xg_w[:].bitcast(E4M3), rhs_scale=xg_s[:], start=(t % 2 == 0), stop=False,
            )
        for t in range(PACK):
            nc.tensor.matmul_mx(
                out=b_banks[t // 2][:, t % 2, :], lhsT=w0d_w[:, t, :].bitcast(E5M2), lhsT_scale=w0d_s[:, t, :],
                rhs=og_w[:].bitcast(E2M1), rhs_scale=og_s[:], start=False, stop=(t % 2 == 1),
            )
        b_rows = [sbuf("b_rows%d" % t, [P, J], F32) for t in range(PACK)]
        for t in range(PACK):
            nc.vector.tensor_copy(b_rows[t][:], b_banks[t // 2][:, t % 2, :])

        pages = [sbuf("page%d" % h, [P, E], F32, tag=tag) for h, tag in enumerate(("w2_w", "w0d_s"))]
        for zeroed in pages:
            nc.vector.memset(zeroed[:].bitcast(I32), 0)

        larger = sbuf("larger", [P, PACK, O], F32, tag="w0d_w")
        for u in range(2):
            ts = slice(2 * u, 2 * u + 2)
            nc.vector.tensor_tensor(larger[:, ts, :], first[:, ts, :], second[:, ts, :], MAX)

        third = sbuf("third", [P, PACK, O], F32)
        hid = sbuf("hid", [P, O, PACK], BF16)

        def look_up_b(t, places):
            entries = l_slot[:, places.start // 16 : places.stop // 16]
            nc.scalar.activation(third[:, t, places], b_rows[t][:].indirect(entries), COPY, scale=sd_t[:, t : t + 1])

        def take_off(ts, places):
            nc.vector.tensor_tensor(
                hid[:, places, ts],
                larger[:, ts, places].rearrange("p t o -> p o t"),
                third[:, ts, places].rearrange("p t o -> p o t"),
                SUB,
            )

        for t in range(PACK - 1):
            look_up_b(t, slice(0, O))
        take_off(slice(0, 2), slice(0, O))
        for places in (slice(0, O // 2), slice(O // 2, O)):
            look_up_b(PACK - 1, places)
            take_off(slice(2, PACK), places)
        hid_w = sbuf("hid_w", [P, O], U32)
        hid_s = sbuf("hid_s", [P, O], U8)
        nc.vector.quantize_mx(out=hid_w[:].bitcast(E4M3), scales=hid_s[:], in_=hid[:].rearrange("p o t -> p (o t)"))

        p_banks = [psum.tile([P, O], F32, name="p_bank%d" % h) for h in range(N // P)]
        p_rows = [sbuf("p_rows%d" % h, [P, O], F32) for h in range(N // P)]
        for h in range(N // P):
            cols = slice(h * P, (h + 1) * P)
            nc.tensor.matmul_mx(
                out=p_banks[h][:], lhsT=wb_w[:, cols].bitcast(E5M2), lhsT_scale=wb_s[:, cols],
                rhs=hid_w[:].bitcast(E4M3), rhs_scale=hid_s[:], start=True, stop=True,
            )
        nc.scalar.copy(p_rows[0][:], p_banks[0][:])
        nc.scalar.activation(pages[0][:].indirect(l_page[:]), p_rows[0][:], COPY)
        nc.vector.tensor_copy(p_rows[1][:], p_banks[1][:])
        nc.vector.tensor_copy(pages[1][:].indirect(l_page[:]), p_rows[1][:])
        for h, queue in enumerate((nc.scalar, nc.sync)):
            queue.dma_start(out[h * P : (h + 1) * P, :], pages[h][:])
